import numpy as np
CORES = [11,27,43,59,75,91,107,123]
N = 8
def setup_inputs(rng):
    return {"x1": rng.standard_normal((N, 128, 8), dtype=np.float32), "x2": rng.standard_normal((N, 128, 256), dtype=np.float32)}
def reference(x1, x2):
    out = []
    s = x1.sum(axis=0, dtype=np.float64).astype(x1.dtype)
    b = 8 // N
    out.append(np.stack([s[:, r * b:(r + 1) * b] for r in range(N)]))
    out.append(np.broadcast_to(x2[4], x2.shape))
    return {"y1": out[0], "y2": out[1]}

@@ -1,0 +1,98 @@
+from concourse.bass import DstId, RemoteDMATransfer
+
+NP = 16
+NA = 10
+
+SCRATCH = {
+    "land": ("dram", [64 + NP * 128, 16], "float32"),
+    "x1p": ("dram", [128, 16], "float32"),
+    "xs": ("dram", [8, 128, 16], "float32"),
+    "sp": ("dram", [128, 16], "float32"),
+}
+SEMAPHORES = ["ldA", "ldB", "pc", "xa", "arrE", "arrL", "rs", "sent", "st", "gy"]
+
+
+def rank_program(g, core, T, topo):
+    cores = list(T.cores)
+    root = cores[4]
+    others = [c for c in cores if c != root]
+    S = T.sem
+
+    def did(c):
+        rid, pid, _se = topo.addr(c)
+        return DstId(rid=rid, pnc=pid)
+
+    def pieces(a, b):
+        return T.land[64 + 128 * a:64 + 128 * b, :]
+
+    def send(p, dst, mask, sem):
+        return RemoteDMATransfer(dst_ids=[did(dst)], dma_engine_mask=mask, remote_sem=sem,
+                                 src=pieces(p, p + 1), dst=pieces(p, p + 1))
+
+    fw = {}
+    for i, rc in enumerate(others[:4]):
+        fw[2 * i] = rc - 1
+        fw[2 * i + 1] = rc + 3
+    fw[8] = root + 3
+    fw[9] = root + 4
+    for i, rc in enumerate(others[4:]):
+        fw[10 + 2 * i] = rc - 1
+        fw[11 + 2 * i] = rc + 3
+    folder = root - 1
+    piece_of = {c: p for p, c in fw.items()}
+
+    rank = T.rank_of(core)
+
+    if core in piece_of:
+        p = piece_of[core]
+        g.wait_ge(S.pc, 2 if p in (8, 9) else 1)
+        sem = S.arrE if p < NA else S.arrL
+        g.remote_dma_fused([send(p, d, 1 << i, sem) for i, d in enumerate(others)], local_sem=S.sent)
+        g.wait_ge(S.sent, len(others))
+        return
+
+    if core == folder:
+        g.wait_ge(S.xa, 7 * 8 + 4)
+        tr = RemoteDMATransfer(dst_ids=[did(d) for d in cores], dma_engine_mask=0xFF, remote_sem=S.rs,
+                               srcs=[T.xs[k] for k in range(8)], dsts=[T.sp[:] for _d in cores], alu_op=1)
+        g.remote_dma_fused([tr], local_sem=S.sent)
+        g.wait_ge(S.sent, 8)
+        return
+
+    if rank is None:
+        return
+
+    if core == root:
+        g.sync.dma_start(pieces(0, NA), T.x2[0:8 * NA, :]).then_inc(S.ldA, 16)
+        g.scalar.dma_start(T.land[0:64, :], T.x1[:]).then_inc(S.ldA, 16)
+        g.scalar.dma_start(pieces(NA, NP), T.x2[8 * NA:128, :]).then_inc(S.ldB, 16)
+        g.wait_ge(S.ldA, 32)
+        trs = [send(p, fw[p], 1 << p, S.pc) for p in range(8)]
+        trs.append(send(8, fw[8], 0x0300, S.pc))
+        trs.append(send(9, fw[9], 0x0C00, S.pc))
+        trs.append(RemoteDMATransfer(dst_ids=[did(folder)], dma_engine_mask=0xF000, remote_sem=S.xa,
+                                     src=T.land[0:128, :], dst=T.xs[rank]))
+        g.remote_dma_fused(trs, local_sem=S.sent)
+        g.wait_ge(S.ldB, 16)
+        g.remote_dma_fused([send(p, fw[p], 1 << (p - NA), S.pc) for p in range(NA, NP)], local_sem=S.sent)
+        g.sync.wait_ge(S.sent, 8 + 2 + 2 + 4 + (NP - NA))
+        g.sync.dma_start(T.y2[:], T.x2[:]).then_inc(S.st, 16)
+        n_st = 16
+    else:
+        g.sync.dma_start(T.x1p[0:64, :], T.x1[:]).then_inc(S.ldA, 16)
+        g.scalar.dma_start(T.x1p[64:128, :], T.x1[:]).then_inc(S.ldA, 16)
+        g.wait_ge(S.ldA, 32)
+        rid, pid, _se = topo.addr(folder)
+        g.remote_dma(T.xs[rank], T.x1p[:], S.xa, S.sent, pid, rid, 0xFF)
+        g.sync.wait_ge(S.arrE, NA)
+        g.sync.dma_start(T.y2[0:8 * NA, :], pieces(0, NA)).then_inc(S.st, 16)
+        g.scalar.wait_ge(S.arrL, NP - NA)
+        g.scalar.dma_start(T.y2[8 * NA:128, :], pieces(NA, NP)).then_inc(S.st, 16)
+        n_st = 32
+
+    g.wait_ge(S.rs, 8)
+    g.dma_start(T.y1[:], T.sp[0:64, rank:16:8], allow_slow_non_contiguous=True).then_inc(S.gy, 16)
+    g.wait_ge(S.gy, 16)
+    if core != root:
+        g.wait_ge(S.sent, 8)
+    g.sync.wait_ge(S.st, n_st)

@@ -4,12 +4,12 @@ NP = 16
 NA = 10
 
 SCRATCH = {
-    "land": ("dram", [64 + NP * 128, 16], "float32"),
-    "x1p": ("dram", [128, 16], "float32"),
-    "xs": ("dram", [8, 128, 16], "float32"),
-    "sp": ("dram", [128, 16], "float32"),
+    "land": ("dram", [NP * 128, 16], "float32"),
+    "x1c": ("dram", [128, 8], "float32"),
+    "xs": ("dram", [8, 128, 8], "float32"),
+    "sb": ("sbuf", [128, 8], "float32"),
 }
-SEMAPHORES = ["ldA", "ldB", "pc", "xa", "arrE", "arrL", "rs", "sent", "st", "gy"]
+SEMAPHORES = ["ldX", "ldA", "ldB", "pc", "xa", "arrE", "arrL", "rs", "sent", "st"]
 
 
 def rank_program(g, core, T, topo):
@@ -23,11 +23,11 @@ def rank_program(g, core, T, topo):
         return DstId(rid=rid, pnc=pid)
 
     def pieces(a, b):
-        return T.land[64 + 128 * a:64 + 128 * b, :]
+        return T.land[128 * a:128 * b, :]
 
-    def send(p, dst, mask, sem):
-        return RemoteDMATransfer(dst_ids=[did(dst)], dma_engine_mask=mask, remote_sem=sem,
-                                 src=pieces(p, p + 1), dst=pieces(p, p + 1))
+    def send(p, dsts, mask, sem):
+        return RemoteDMATransfer(dst_ids=[did(d) for d in dsts], dma_engine_mask=mask, remote_sem=sem,
+                                 srcs=[pieces(p, p + 1)], dsts=[pieces(p, p + 1) for _d in dsts])
 
     fw = {}
     for i, rc in enumerate(others[:4]):
@@ -38,61 +38,64 @@ def rank_program(g, core, T, topo):
     for i, rc in enumerate(others[4:]):
         fw[10 + 2 * i] = rc - 1
         fw[11 + 2 * i] = rc + 3
-    folder = root - 1
     piece_of = {c: p for p, c in fw.items()}
+    folders = [c - 2 for c in cores]
 
     rank = T.rank_of(core)
 
     if core in piece_of:
         p = piece_of[core]
-        g.wait_ge(S.pc, 2 if p in (8, 9) else 1)
+        g.wait_ge(S.pc, 4 if p in (8, 9) else 1)
         sem = S.arrE if p < NA else S.arrL
-        g.remote_dma_fused([send(p, d, 1 << i, sem) for i, d in enumerate(others)], local_sem=S.sent)
-        g.wait_ge(S.sent, len(others))
+        far = [d for d in others if topo.chip(d) != topo.chip(core)]
+        near = [d for d in others if topo.chip(d) == topo.chip(core)]
+        trs = [send(p, far, 0x00FF, sem)]
+        if near:
+            trs.append(send(p, near, 0xFF00, sem))
+        g.remote_dma_fused(trs, local_sem=S.sent)
+        g.wait_ge(S.sent, 8 * len(trs))
         return
 
-    if core == folder:
-        g.wait_ge(S.xa, 7 * 8 + 4)
-        tr = RemoteDMATransfer(dst_ids=[did(d) for d in cores], dma_engine_mask=0xFF, remote_sem=S.rs,
-                               srcs=[T.xs[k] for k in range(8)], dsts=[T.sp[:] for _d in cores], alu_op=1)
+    if core in folders:
+        g.wait_ge(S.xa, 8 * 8)
+        tr = RemoteDMATransfer(dst_ids=[did(core + 2)], dma_engine_mask=0xFFFF, remote_sem=S.rs,
+                               srcs=[T.xs[k] for k in range(8)], dsts=[T.sb[:]], alu_op=1)
         g.remote_dma_fused([tr], local_sem=S.sent)
-        g.wait_ge(S.sent, 8)
+        g.wait_ge(S.sent, 16)
         return
 
     if rank is None:
         return
 
+    x1_out = RemoteDMATransfer(dst_ids=[did(f) for f in folders], dma_engine_mask=0x00FF, remote_sem=S.xa,
+                               srcs=[T.x1c[:]], dsts=[T.xs[rank] for _f in folders])
     if core == root:
+        g.scalar.dma_start(T.x1c[:], T.x1[:]).then_inc(S.ldX, 16)
         g.sync.dma_start(pieces(0, NA), T.x2[0:8 * NA, :]).then_inc(S.ldA, 16)
-        g.scalar.dma_start(T.land[0:64, :], T.x1[:]).then_inc(S.ldA, 16)
         g.scalar.dma_start(pieces(NA, NP), T.x2[8 * NA:128, :]).then_inc(S.ldB, 16)
-        g.wait_ge(S.ldA, 32)
-        trs = [send(p, fw[p], 1 << p, S.pc) for p in range(8)]
-        trs.append(send(8, fw[8], 0x0300, S.pc))
-        trs.append(send(9, fw[9], 0x0C00, S.pc))
-        trs.append(RemoteDMATransfer(dst_ids=[did(folder)], dma_engine_mask=0xF000, remote_sem=S.xa,
-                                     src=T.land[0:128, :], dst=T.xs[rank]))
+        g.wait_ge(S.ldX, 16)
+        g.remote_dma_fused([x1_out], local_sem=S.sent)
+        g.wait_ge(S.ldA, 16)
+        trs = [send(p, [fw[p]], 1 << p, S.pc) for p in range(8)]
+        trs.append(send(8, [fw[8]], 0x0F00, S.pc))
+        trs.append(send(9, [fw[9]], 0xF000, S.pc))
         g.remote_dma_fused(trs, local_sem=S.sent)
         g.wait_ge(S.ldB, 16)
-        g.remote_dma_fused([send(p, fw[p], 1 << (p - NA), S.pc) for p in range(NA, NP)], local_sem=S.sent)
-        g.sync.wait_ge(S.sent, 8 + 2 + 2 + 4 + (NP - NA))
-        g.sync.dma_start(T.y2[:], T.x2[:]).then_inc(S.st, 16)
-        n_st = 16
-    else:
-        g.sync.dma_start(T.x1p[0:64, :], T.x1[:]).then_inc(S.ldA, 16)
-        g.scalar.dma_start(T.x1p[64:128, :], T.x1[:]).then_inc(S.ldA, 16)
-        g.wait_ge(S.ldA, 32)
-        rid, pid, _se = topo.addr(folder)
-        g.remote_dma(T.xs[rank], T.x1p[:], S.xa, S.sent, pid, rid, 0xFF)
-        g.sync.wait_ge(S.arrE, NA)
-        g.sync.dma_start(T.y2[0:8 * NA, :], pieces(0, NA)).then_inc(S.st, 16)
-        g.scalar.wait_ge(S.arrL, NP - NA)
-        g.scalar.dma_start(T.y2[8 * NA:128, :], pieces(NA, NP)).then_inc(S.st, 16)
+        g.remote_dma_fused([send(p, [fw[p]], 1 << (p - NA), S.pc) for p in range(NA, NP)], local_sem=S.sent)
+        g.scalar.wait_ge(S.sent, 8 + 8 + 4 + 4 + (NP - NA))
+        g.scalar.dma_start(T.y2[:], T.x2[:]).then_inc(S.st, 16)
         n_st = 32
-
-    g.wait_ge(S.rs, 8)
-    g.dma_start(T.y1[:], T.sp[0:64, rank:16:8], allow_slow_non_contiguous=True).then_inc(S.gy, 16)
-    g.wait_ge(S.gy, 16)
-    if core != root:
+    else:
+        g.sync.dma_start(T.x1c[:], T.x1[:]).then_inc(S.ldX, 16)
+        g.wait_ge(S.ldX, 16)
+        g.remote_dma_fused([x1_out], local_sem=S.sent)
         g.wait_ge(S.sent, 8)
+        g.sync.wait_ge(S.arrE, 8 * NA)
+        g.sync.dma_start(T.y2[0:8 * NA, :], pieces(0, NA)).then_inc(S.st, 16)
+        g.scalar.wait_ge(S.arrL, 8 * (NP - NA))
+        g.scalar.dma_start(T.y2[8 * NA:128, :], pieces(NA, NP)).then_inc(S.st, 16)
+        n_st = 48
+
+    g.sync.wait_ge(S.rs, 16)
+    g.sync.dma_start(T.y1[:], T.sb[:, rank:rank + 1]).then_inc(S.st, 16)
     g.sync.wait_ge(S.st, n_st)

from concourse.bass import DstId, RemoteDMATransfer

NP = 16
NA = 10

SCRATCH = {
    "land": ("dram", [NP * 128, 16], "float32"),
    "x1c": ("dram", [128, 8], "float32"),
    "xs": ("dram", [8, 128, 8], "float32"),
    "sb": ("sbuf", [128, 8], "float32"),
}
SEMAPHORES = ["ldX", "ldA", "ldB", "pc", "xa", "arrE", "arrL", "rs", "sent", "st"]


def rank_program(g, core, T, topo):
    cores = list(T.cores)
    root = cores[4]
    others = [c for c in cores if c != root]
    S = T.sem

    def did(c):
        rid, pid, _se = topo.addr(c)
        return DstId(rid=rid, pnc=pid)

    def pieces(a, b):
        return T.land[128 * a:128 * b, :]

    def send(p, dsts, mask, sem):
        return RemoteDMATransfer(dst_ids=[did(d) for d in dsts], dma_engine_mask=mask, remote_sem=sem,
                                 srcs=[pieces(p, p + 1)], dsts=[pieces(p, p + 1) for _d in dsts])

    fw = {}
    for i, rc in enumerate(others[:4]):
        fw[2 * i] = rc - 1
        fw[2 * i + 1] = rc + 3
    fw[8] = root + 3
    fw[9] = root + 4
    for i, rc in enumerate(others[4:]):
        fw[10 + 2 * i] = rc - 1
        fw[11 + 2 * i] = rc + 3
    piece_of = {c: p for p, c in fw.items()}
    folders = [c - 2 for c in cores]

    rank = T.rank_of(core)

    if core in piece_of:
        p = piece_of[core]
        g.wait_ge(S.pc, 4 if p in (8, 9) else 1)
        sem = S.arrE if p < NA else S.arrL
        far = [d for d in others if topo.chip(d) != topo.chip(core)]
        near = [d for d in others if topo.chip(d) == topo.chip(core)]
        trs = [send(p, far, 0x00FF, sem)]
        if near:
            trs.append(send(p, near, 0xFF00, sem))
        g.remote_dma_fused(trs, local_sem=S.sent)
        g.wait_ge(S.sent, 8 * len(trs))
        return

    if core in folders:
        g.wait_ge(S.xa, 8 * 8)
        tr = RemoteDMATransfer(dst_ids=[did(core + 2)], dma_engine_mask=0xFFFF, remote_sem=S.rs,
                               srcs=[T.xs[k] for k in range(8)], dsts=[T.sb[:]], alu_op=1)
        g.remote_dma_fused([tr], local_sem=S.sent)
        g.wait_ge(S.sent, 16)
        return

    if rank is None:
        return

    x1_out = RemoteDMATransfer(dst_ids=[did(f) for f in folders], dma_engine_mask=0x00FF, remote_sem=S.xa,
                               srcs=[T.x1c[:]], dsts=[T.xs[rank] for _f in folders])
    if core == root:
        g.scalar.dma_start(T.x1c[:], T.x1[:]).then_inc(S.ldX, 16)
        g.sync.dma_start(pieces(0, NA), T.x2[0:8 * NA, :]).then_inc(S.ldA, 16)
        g.scalar.dma_start(pieces(NA, NP), T.x2[8 * NA:128, :]).then_inc(S.ldB, 16)
        g.wait_ge(S.ldX, 16)
        g.remote_dma_fused([x1_out], local_sem=S.sent)
        g.wait_ge(S.ldA, 16)
        trs = [send(p, [fw[p]], 1 << p, S.pc) for p in range(8)]
        trs.append(send(8, [fw[8]], 0x0F00, S.pc))
        trs.append(send(9, [fw[9]], 0xF000, S.pc))
        g.remote_dma_fused(trs, local_sem=S.sent)
        g.wait_ge(S.ldB, 16)
        g.remote_dma_fused([send(p, [fw[p]], 1 << (p - NA), S.pc) for p in range(NA, NP)], local_sem=S.sent)
        g.scalar.wait_ge(S.sent, 8 + 8 + 4 + 4 + (NP - NA))
        g.scalar.dma_start(T.y2[:], T.x2[:]).then_inc(S.st, 16)
        n_st = 32
    else:
        g.sync.dma_start(T.x1c[:], T.x1[:]).then_inc(S.ldX, 16)
        g.wait_ge(S.ldX, 16)
        g.remote_dma_fused([x1_out], local_sem=S.sent)
        g.wait_ge(S.sent, 8)
        g.sync.wait_ge(S.arrE, 8 * NA)
        g.sync.dma_start(T.y2[0:8 * NA, :], pieces(0, NA)).then_inc(S.st, 16)
        g.scalar.wait_ge(S.arrL, 8 * (NP - NA))
        g.scalar.dma_start(T.y2[8 * NA:128, :], pieces(NA, NP)).then_inc(S.st, 16)
        n_st = 48

    g.sync.wait_ge(S.rs, 16)
    g.sync.dma_start(T.y1[:], T.sb[:, rank:rank + 1]).then_inc(S.st, 16)
    g.sync.wait_ge(S.st, n_st)
